import numpy as np
import ml_dtypes


def mxq(x, axis, fmt="e4m3"):
    dtype, down = {"e4m3": (ml_dtypes.float8_e4m3fn, 7), "e5m2": (ml_dtypes.float8_e5m2, 14)}[fmt]
    v = np.moveaxis(np.asarray(x, np.float32).astype(ml_dtypes.bfloat16).astype(np.float64), axis, -1)
    blocks = v.reshape(v.shape[:-1] + (-1, 32))
    amax = np.abs(blocks).max(-1, keepdims=True)
    byte = np.maximum(np.where(amax > 0, np.frexp(amax)[1] - 1 + 127, 0) - down, 1)
    scale = np.exp2(byte - 127.0)
    codes = (blocks / scale).astype(np.float32).astype(dtype).astype(np.float64)
    return np.moveaxis((codes * scale).reshape(v.shape), -1, axis)


WIDE = False


def mx_kscale(k):
    if not WIDE:
        return np.ones(k)
    levels = np.array([10, -10, 5, -5, 0])
    if k % 512:
        return np.exp2(np.random.permutation(np.resize(levels, k // 32))).repeat(32)
    a = np.empty((k // 512, 16))
    for p in range(k // 512):
        a[p, :8] = np.random.permutation(np.resize(levels, 8))
        for g in range(8):
            far = levels[np.abs(levels - a[p, g]) >= 10]
            a[p, g + 8] = far[np.random.randint(len(far))]
    return np.exp2(a.ravel()).repeat(32)


def f64(x):
    return np.asarray(x).astype(np.float64)


def striped(idx):
    return np.tile(idx.reshape(-1, 16).T, (8, 1)).astype(np.uint16)


def unstriped(offs):
    return offs[:16].T.reshape(-1).astype(np.int64)


E2M1 = np.array([0.0, 0.5, 1.0, 1.5, 2.0, 3.0, 4.0, 6.0, -0.0, -0.5, -1.0, -1.5, -2.0, -3.0, -4.0, -6.0])


def pack_fp4(w):
    k, n = w.shape
    w = f64(np.asarray(w, np.float32).astype(ml_dtypes.bfloat16)).reshape(k // 32, 32, n)
    amax = np.abs(w).max(1)
    mant, ex = np.frexp(amax / 6.0)
    byte = np.clip(np.where(amax > 0, np.where(mant > 0.5, ex, ex - 1) + 127, 1), 1, 254)
    scaled = (w * np.exp2(127.0 - byte)[:, None, :]).reshape(k, n).astype(np.float32)
    c = np.ascontiguousarray(scaled.reshape(k // 512, 128, 4, n).transpose(0, 1, 3, 2)).astype(ml_dtypes.float4_e2m1fn).view(np.uint8) & 0xF
    words = (c[..., 0::2] | (c[..., 1::2] << 4)).reshape(k // 512, 128, 2 * n)
    return np.ascontiguousarray(words), np.ascontiguousarray(byte.astype(np.uint8).reshape(k // 512, 16, n))


def unpack_fp4(words, scales):
    g, _, n = scales.shape
    words = np.ascontiguousarray(words).reshape(g, 128, n, 2)
    nib = np.empty((g, 128, n, 4), np.uint8)
    nib[..., 0::2] = words & 0xF
    nib[..., 1::2] = words >> 4
    vals = E2M1[nib] * np.repeat(np.exp2(scales.astype(np.float64) - 127.0), 8, axis=1)[..., None]
    return vals.transpose(0, 1, 3, 2).reshape(g * 512, n)


def relu(v):
    return np.maximum(v, 0.0)


K, T, N = 512, 512, 128


def setup_inputs():
    n = np.random.standard_normal
    s = mx_kscale(K)[:, None]
    packed_xT = pack_fp4(n((K, T)) * s)
    return {
        "x_words": packed_xT[0],
        "x_scales": packed_xT[1],
        "w1": (n((K, N)) / np.sqrt(K) / s).astype(np.float32),
        "pos1": striped(np.random.permutation(T)),
        "pos2": striped(np.random.permutation(T)),
        "pos3": striped(np.random.permutation(T)),
    }


def reference(x_words, x_scales, w1, pos1, pos2, pos3):
    xq = unpack_fp4(x_words, x_scales)
    y = relu(mxq(f64(w1), 0, "e4m3").T @ xq)
    n0 = y[:, unstriped(pos1)]
    n1 = y[:, unstriped(pos2)]
    n2 = y[:, unstriped(pos3)]
    return np.maximum(np.minimum(n0, n1), np.minimum(np.maximum(n0, n1), n2))

@@ -1,0 +1,124 @@
+from contextlib import ExitStack
+
+import concourse.mybir as mybir
+
+K, T, N = 512, 512, 128
+FLOPS = 2 * K * T * N
+
+F32 = mybir.dt.float32
+BF16 = mybir.dt.bfloat16
+I32 = mybir.dt.int32
+U32 = mybir.dt.uint32
+U16 = mybir.dt.uint16
+U8 = mybir.dt.uint8
+FP8X4 = mybir.dt.float8_e4m3fn_x4
+FP4X4 = mybir.dt.float4_e2m1fn_x4
+MAX = mybir.AluOpType.max
+MIN = mybir.AluOpType.min
+RELU = mybir.ActivationFunctionType.Relu
+
+P = 128
+PACK = 4
+HALF = T // 2
+CHUNKS = ((0, 192), (192, 384), (384, 512))
+
+
+def tile_picked_wmedian_relu_l_kernel(tc, x_words, x_scales, w1, pos1, pos2, pos3, out):
+    nc = tc.nc
+    with ExitStack() as ctx:
+        keep = ctx.enter_context(tc.tile_pool(name="keep", bufs=1))
+        psum = ctx.enter_context(tc.psum_pool(name="psum", bufs=1))
+
+        x_plane = keep.tile([P, T], U8, name="x_plane", align_bytes=64)
+        nc.vector.memset(x_plane[:].bitcast(I32), 0)
+
+        w_raw = keep.tile([P, PACK, N], F32, name="w_raw")
+        nc.sync.dma_start(out=w_raw[:], in_=w1.rearrange("(p j) m -> p j m", j=PACK))
+        x_codes = keep.tile([P, 2 * T], U8, name="x_codes", align_bytes=64)
+        nc.sync.dma_start(out=x_codes[:].bitcast(I32), in_=x_words[0].bitcast(I32))
+        for q in range(4):
+            nc.sync.dma_start(
+                out=x_plane[32 * q : 32 * q + 4, :].bitcast(I32),
+                in_=x_scales[0, 4 * q : 4 * q + 4, :].bitcast(I32),
+            )
+        lists = []
+        for name, pos in (("pos1", pos1), ("pos2", pos2), ("pos3", pos3)):
+            offsets = keep.tile([P, T // 16], U16, name=name)
+            nc.sync.dma_start(offsets[:], pos)
+            lists.append(offsets)
+
+        w_grouped = keep.tile([P, N, PACK], BF16, name="w_grouped", align_bytes=64)
+        nc.vector.tensor_copy(
+            out=w_grouped[:].rearrange("p (c i) t -> p c t i", i=4),
+            in_=w_raw[:].rearrange("p t (c i) -> p c t i", i=4),
+        )
+        w_codes = keep.tile([P, N], U32, name="w_codes", align_bytes=64)
+        w_plane = keep.tile([P, N], U8, name="w_plane", align_bytes=64)
+        nc.vector.quantize_mx(
+            out=w_codes[:].bitcast(FP8X4),
+            scales=w_plane[:],
+            in_=w_grouped[:].rearrange("p m t -> p (m t)"),
+        )
+
+        y = keep.tile([P, T], F32, name="y")
+        for h in range(2):
+            cols = slice(h * HALF, (h + 1) * HALF)
+            acc = psum.tile([P, HALF], F32, name="acc%d" % h)
+            nc.tensor.matmul_mx(
+                out=acc[:],
+                lhsT=w_codes[:].bitcast(FP8X4),
+                lhsT_scale=w_plane[:],
+                rhs=x_codes[:, 2 * cols.start : 2 * cols.stop].bitcast(FP4X4),
+                rhs_scale=x_plane[:, cols],
+                start=True,
+                stop=True,
+            )
+            if h == 0:
+                nc.vector.tensor_scalar_max(out=y[:, cols], in0=acc[:], scalar1=0.0)
+            else:
+                nc.scalar.activation(out=y[:, cols], in_=acc[:], func=RELU)
+
+        def tiles(tag):
+            return [keep.tile([P, b - a], F32, name="%s%d" % (tag, a)) for a, b in CHUNKS]
+
+        n0, n1, n2, hi, lo, mid, med = (tiles(t) for t in ("a", "b", "c", "hi", "lo", "mid", "med"))
+
+        def gather(dst, d, c):
+            a, b = CHUNKS[c]
+            nc.vector.tensor_copy(out=dst[c][:], in_=y[:].indirect(lists[d][:, a // 16 : b // 16]))
+
+        def upper(c):
+            nc.vector.tensor_tensor(out=hi[c][:], in0=n0[c][:], in1=n1[c][:], op=MAX)
+
+        def lower(c):
+            nc.vector.tensor_tensor(out=lo[c][:], in0=n0[c][:], in1=n1[c][:], op=MIN)
+
+        def middle(c):
+            nc.vector.tensor_tensor(out=mid[c][:], in0=hi[c][:], in1=n2[c][:], op=MIN)
+
+        def finish(c, queue):
+            a, b = CHUNKS[c]
+            nc.vector.tensor_tensor(out=med[c][:], in0=lo[c][:], in1=mid[c][:], op=MAX)
+            queue.dma_start(out=out[:, a:b], in_=med[c][:])
+
+        gather(n0, 0, 0)
+        gather(n1, 1, 0)
+        gather(n2, 2, 0)
+        upper(0)
+        lower(0)
+        gather(n0, 0, 1)
+        middle(0)
+        gather(n1, 1, 1)
+        finish(0, nc.sync)
+        gather(n2, 2, 1)
+        upper(1)
+        gather(n0, 0, 2)
+        lower(1)
+        gather(n1, 1, 2)
+        middle(1)
+        gather(n2, 2, 2)
+        upper(2)
+        lower(2)
+        middle(2)
+        finish(1, nc.scalar)
+        finish(2, nc.sync)

@@ -60,10 +60,11 @@ def tile_picked_wmedian_relu_l_kernel(tc, x_words, x_scales, w1, pos1, pos2, pos
             in_=w_grouped[:].rearrange("p m t -> p (m t)"),
         )
 
-        y = keep.tile([P, T], F32, name="y")
-        for h in range(2):
-            cols = slice(h * HALF, (h + 1) * HALF)
-            acc = psum.tile([P, HALF], F32, name="acc%d" % h)
+        y = keep.tile([P, 2 * T], F32, name="y")
+        nc.vector.memset(y[:, T:], 0.0)
+        for h, (a, b, eng) in enumerate(((0, 128, "v"), (128, 256, "s"), (256, 384, "v"), (384, 512, "s"))):
+            cols = slice(a, b)
+            acc = psum.tile([P, b - a], F32, name="acc%d" % h)
             nc.tensor.matmul_mx(
                 out=acc[:],
                 lhsT=w_codes[:].bitcast(FP8X4),
@@ -73,52 +74,29 @@ def tile_picked_wmedian_relu_l_kernel(tc, x_words, x_scales, w1, pos1, pos2, pos
                 start=True,
                 stop=True,
             )
-            if h == 0:
+            if eng == "v":
                 nc.vector.tensor_scalar_max(out=y[:, cols], in0=acc[:], scalar1=0.0)
             else:
                 nc.scalar.activation(out=y[:, cols], in_=acc[:], func=RELU)
 
-        def tiles(tag):
-            return [keep.tile([P, b - a], F32, name="%s%d" % (tag, a)) for a, b in CHUNKS]
-
-        n0, n1, n2, hi, lo, mid, med = (tiles(t) for t in ("a", "b", "c", "hi", "lo", "mid", "med"))
-
-        def gather(dst, d, c):
-            a, b = CHUNKS[c]
-            nc.vector.tensor_copy(out=dst[c][:], in_=y[:].indirect(lists[d][:, a // 16 : b // 16]))
-
-        def upper(c):
-            nc.vector.tensor_tensor(out=hi[c][:], in0=n0[c][:], in1=n1[c][:], op=MAX)
-
-        def lower(c):
-            nc.vector.tensor_tensor(out=lo[c][:], in0=n0[c][:], in1=n1[c][:], op=MIN)
+        n0, n1, n2, hi, lo, mid, med = (keep.tile([P, T], F32, name=t) for t in ("a", "b", "c", "hi", "lo", "mid", "med"))
+        for dst, offsets in zip((n0, n1, n2), lists):
+            nc.vector.tensor_copy(out=dst[:], in_=y[:].indirect(offsets[:]))
+        nc.vector.tensor_tensor(out=hi[:], in0=n0[:], in1=n1[:], op=MAX)
+        nc.vector.tensor_tensor(out=lo[:], in0=n0[:], in1=n1[:], op=MIN)
 
         def middle(c):
-            nc.vector.tensor_tensor(out=mid[c][:], in0=hi[c][:], in1=n2[c][:], op=MIN)
+            cols = slice(*CHUNKS[c])
+            nc.vector.tensor_tensor(out=mid[:, cols], in0=hi[:, cols], in1=n2[:, cols], op=MIN)
 
         def finish(c, queue):
-            a, b = CHUNKS[c]
-            nc.vector.tensor_tensor(out=med[c][:], in0=lo[c][:], in1=mid[c][:], op=MAX)
-            queue.dma_start(out=out[:, a:b], in_=med[c][:])
+            cols = slice(*CHUNKS[c])
+            nc.vector.tensor_tensor(out=med[:, cols], in0=lo[:, cols], in1=mid[:, cols], op=MAX)
+            queue.dma_start(out=out[:, cols], in_=med[:, cols])
 
-        gather(n0, 0, 0)
-        gather(n1, 1, 0)
-        gather(n2, 2, 0)
-        upper(0)
-        lower(0)
-        gather(n0, 0, 1)
         middle(0)
-        gather(n1, 1, 1)
-        finish(0, nc.sync)
-        gather(n2, 2, 1)
-        upper(1)
-        gather(n0, 0, 2)
-        lower(1)
-        gather(n1, 1, 2)
         middle(1)
-        gather(n2, 2, 2)
-        upper(2)
-        lower(2)
+        finish(0, nc.sync)
         middle(2)
         finish(1, nc.scalar)
         finish(2, nc.sync)

@@ -98,5 +98,5 @@ def tile_picked_wmedian_relu_l_kernel(tc, x_words, x_scales, w1, pos1, pos2, pos
         middle(1)
         finish(0, nc.sync)
         middle(2)
-        finish(1, nc.scalar)
+        finish(1, nc.sync)
         finish(2, nc.sync)

@@ -32,8 +32,12 @@ def tile_picked_wmedian_relu_l_kernel(tc, x_words, x_scales, w1, pos1, pos2, pos
         x_plane = keep.tile([P, T], U8, name="x_plane", align_bytes=64)
         nc.vector.memset(x_plane[:].bitcast(I32), 0)
 
-        w_raw = keep.tile([P, PACK, N], F32, name="w_raw")
-        nc.sync.dma_start(out=w_raw[:], in_=w1.rearrange("(p j) m -> p j m", j=PACK))
+        w_rows = w1.rearrange("(p j) m -> p j m", j=PACK)
+        w_raw = []
+        for u in range(2):
+            pair = keep.tile([P, 2, N], F32, name="w_raw%d" % u)
+            nc.sync.dma_start(out=pair[:], in_=w_rows[:, 2 * u : 2 * u + 2, :])
+            w_raw.append(pair)
         x_codes = keep.tile([P, 2 * T], U8, name="x_codes", align_bytes=64)
         nc.sync.dma_start(out=x_codes[:].bitcast(I32), in_=x_words[0].bitcast(I32))
         for q in range(4):
@@ -48,17 +52,20 @@ def tile_picked_wmedian_relu_l_kernel(tc, x_words, x_scales, w1, pos1, pos2, pos
             lists.append(offsets)
 
         w_grouped = keep.tile([P, N, PACK], BF16, name="w_grouped", align_bytes=64)
-        nc.vector.tensor_copy(
-            out=w_grouped[:].rearrange("p (c i) t -> p c t i", i=4),
-            in_=w_raw[:].rearrange("p t (c i) -> p c t i", i=4),
-        )
         w_codes = keep.tile([P, N], U32, name="w_codes", align_bytes=64)
         w_plane = keep.tile([P, N], U8, name="w_plane", align_bytes=64)
-        nc.vector.quantize_mx(
-            out=w_codes[:].bitcast(FP8X4),
-            scales=w_plane[:],
-            in_=w_grouped[:].rearrange("p m t -> p (m t)"),
-        )
+        halves = (slice(0, N // 2), slice(N // 2, N))
+        for u, m in ((0, slice(0, N)), (1, halves[0]), (1, halves[1])):
+            nc.vector.tensor_copy(
+                out=w_grouped[:, m, 2 * u : 2 * u + 2].rearrange("p (c i) t -> p c t i", i=4),
+                in_=w_raw[u][:, :, m].rearrange("p t (c i) -> p c t i", i=4),
+            )
+        for m in halves:
+            nc.vector.quantize_mx(
+                out=w_codes[:, m].bitcast(FP8X4),
+                scales=w_plane[:, m],
+                in_=w_grouped[:, m, :].rearrange("p m t -> p (m t)"),
+            )
 
         y = keep.tile([P, 2 * T], F32, name="y")
         nc.vector.memset(y[:, T:], 0.0)

@@ -15,6 +15,8 @@ FP8X4 = mybir.dt.float8_e4m3fn_x4
 FP4X4 = mybir.dt.float4_e2m1fn_x4
 MAX = mybir.AluOpType.max
 MIN = mybir.AluOpType.min
+MULT = mybir.AluOpType.mult
+ADD = mybir.AluOpType.add
 RELU = mybir.ActivationFunctionType.Relu
 
 P = 128
@@ -67,7 +69,7 @@ def tile_picked_wmedian_relu_l_kernel(tc, x_words, x_scales, w1, pos1, pos2, pos
                 in_=w_grouped[:, m, :].rearrange("p m t -> p (m t)"),
             )
 
-        y = keep.tile([P, 2 * T], F32, name="y")
+        y = keep.tile([P, 4 * T], F32, name="y")
         nc.vector.memset(y[:, T:], 0.0)
         for h, (a, b, eng) in enumerate(((0, 128, "v"), (128, 256, "s"), (256, 384, "v"), (384, 512, "s"))):
             cols = slice(a, b)
@@ -88,7 +90,7 @@ def tile_picked_wmedian_relu_l_kernel(tc, x_words, x_scales, w1, pos1, pos2, pos
 
         n0, n1, n2, hi, lo, mid, med = (keep.tile([P, T], F32, name=t) for t in ("a", "b", "c", "hi", "lo", "mid", "med"))
         for dst, offsets in zip((n0, n1, n2), lists):
-            nc.vector.tensor_copy(out=dst[:], in_=y[:].indirect(offsets[:]))
+            nc.vector.tensor_scalar(out=dst[:], in0=y[:].indirect(offsets[:]), scalar1=1.0, scalar2=0.0, op0=MULT, op1=ADD)
         nc.vector.tensor_tensor(out=hi[:], in0=n0[:], in1=n1[:], op=MAX)
         nc.vector.tensor_tensor(out=lo[:], in0=n0[:], in1=n1[:], op=MIN)
 

@@ -1,6 +1,7 @@
 from contextlib import ExitStack
 
 import concourse.mybir as mybir
+from concourse.masks import make_identity
 
 K, T, N = 512, 512, 128
 FLOPS = 2 * K * T * N
@@ -17,11 +18,14 @@ MAX = mybir.AluOpType.max
 MIN = mybir.AluOpType.min
 MULT = mybir.AluOpType.mult
 ADD = mybir.AluOpType.add
+SUB = mybir.AluOpType.subtract
+ABS = mybir.ActivationFunctionType.Abs
 RELU = mybir.ActivationFunctionType.Relu
 
 P = 128
 PACK = 4
 HALF = T // 2
+SPARE = 32
 CHUNKS = ((0, 192), (192, 384), (384, 512))
 
 
@@ -53,6 +57,9 @@ def tile_picked_wmedian_relu_l_kernel(tc, x_words, x_scales, w1, pos1, pos2, pos
             nc.sync.dma_start(offsets[:], pos)
             lists.append(offsets)
 
+        ident = keep.tile([P, P], F32, name="ident")
+        make_identity(nc, ident[:])
+
         w_grouped = keep.tile([P, N, PACK], BF16, name="w_grouped", align_bytes=64)
         w_codes = keep.tile([P, N], U32, name="w_codes", align_bytes=64)
         w_plane = keep.tile([P, N], U8, name="w_plane", align_bytes=64)
@@ -69,11 +76,13 @@ def tile_picked_wmedian_relu_l_kernel(tc, x_words, x_scales, w1, pos1, pos2, pos
                 in_=w_grouped[:, m, :].rearrange("p m t -> p (m t)"),
             )
 
-        y = keep.tile([P, 4 * T], F32, name="y")
+        y = keep.tile([P, T + SPARE], F32, name="y")
         nc.vector.memset(y[:, T:], 0.0)
+        minus_one = keep.tile([P, T], F32, name="minus_one")
+        nc.vector.memset(minus_one[:], -1.0)
         for h, (a, b, eng) in enumerate(((0, 128, "v"), (128, 256, "s"), (256, 384, "v"), (384, 512, "s"))):
             cols = slice(a, b)
-            acc = psum.tile([P, b - a], F32, name="acc%d" % h)
+            acc = psum.tile([P, b - a], F32, name="acc%d" % h, tag="bank%d" % h)
             nc.tensor.matmul_mx(
                 out=acc[:],
                 lhsT=w_codes[:].bitcast(FP8X4),
@@ -88,24 +97,50 @@ def tile_picked_wmedian_relu_l_kernel(tc, x_words, x_scales, w1, pos1, pos2, pos
             else:
                 nc.scalar.activation(out=y[:, cols], in_=acc[:], func=RELU)
 
-        n0, n1, n2, hi, lo, mid, med = (keep.tile([P, T], F32, name=t) for t in ("a", "b", "c", "hi", "lo", "mid", "med"))
-        for dst, offsets in zip((n0, n1, n2), lists):
-            nc.vector.tensor_scalar(out=dst[:], in0=y[:].indirect(offsets[:]), scalar1=1.0, scalar2=0.0, op0=MULT, op1=ADD)
-        nc.vector.tensor_tensor(out=hi[:], in0=n0[:], in1=n1[:], op=MAX)
-        nc.vector.tensor_tensor(out=lo[:], in0=n0[:], in1=n1[:], op=MIN)
+        neg0, n1, lo, rise, step, med, gap_t = (
+            keep.tile([P, T], F32, name=t) for t in ("neg0", "n1", "lo", "rise", "step", "med", "gap_t")
+        )
+        blocks = [slice(P * i, P * (i + 1)) for i in range(T // P)]
+        diff = [psum.tile([P, P], F32, name="diff%d" % i) for i in range(T // P)]
+        gap_early = psum.tile([P, T - P], F32, name="gap_early", tag="bank0")
+        gap_late = psum.tile([P, P], F32, name="gap_late", tag="bank1")
+
+        def gap(cols):
+            if cols.start < T - P:
+                return gap_early[:, cols]
+            return gap_late[:, cols.start - (T - P) : cols.stop - (T - P)]
+
+        def entries(window, offsets, cols):
+            return window.indirect(offsets[:, cols.start // 16 : cols.stop // 16])
+
+        sides = (slice(0, HALF), slice(HALF, T))
+        nc.vector.tensor_tensor(out=neg0[:], in0=y[:].indirect(lists[0][:]), in1=minus_one[:], op=MULT)
+        for cols in (slice(0, T - P), slice(T - P, T)):
+            nc.vector.tensor_copy(out=n1[:, cols], in_=entries(y[:], lists[1], cols))
+        for i, cols in enumerate(blocks):
+            nc.tensor.matmul(diff[i][:], lhsT=neg0[:, cols], rhs=ident[:], start=True, stop=False, is_transpose=True)
+        for i, cols in enumerate(blocks):
+            nc.tensor.matmul(diff[i][:], lhsT=n1[:, cols], rhs=ident[:], start=False, stop=True, is_transpose=True)
+        for i, cols in enumerate(blocks):
+            nc.scalar.activation(out=gap_t[:, cols], in_=diff[i][:], func=ABS)
+            nc.tensor.transpose(gap(cols), gap_t[:, cols], ident[:])
+        for cols in sides:
+            nc.vector.scalar_tensor_tensor(out=lo[:, cols], in0=neg0[:, cols], scalar=-1.0, in1=n1[:, cols], op0=MULT, op1=MIN)
+        for cols in sides:
+            nc.vector.tensor_tensor(out=rise[:, cols], in0=entries(y[:], lists[2], cols), in1=lo[:, cols], op=SUB)
 
         def middle(c):
             cols = slice(*CHUNKS[c])
-            nc.vector.tensor_tensor(out=mid[:, cols], in0=hi[:, cols], in1=n2[:, cols], op=MIN)
+            nc.vector.scalar_tensor_tensor(out=step[:, cols], in0=rise[:, cols], scalar=0.0, in1=gap(cols), op0=MAX, op1=MIN)
 
-        def finish(c, queue):
+        def finish(c):
             cols = slice(*CHUNKS[c])
-            nc.vector.tensor_tensor(out=med[:, cols], in0=lo[:, cols], in1=mid[:, cols], op=MAX)
-            queue.dma_start(out=out[:, cols], in_=med[:, cols])
+            nc.vector.tensor_tensor(out=med[:, cols], in0=lo[:, cols], in1=step[:, cols], op=ADD)
+            nc.sync.dma_start(out=out[:, cols], in_=med[:, cols])
 
         middle(0)
         middle(1)
-        finish(0, nc.sync)
+        finish(0)
         middle(2)
-        finish(1, nc.sync)
-        finish(2, nc.sync)
+        finish(1)
+        finish(2)

@@ -45,12 +45,14 @@ def tile_picked_wmedian_relu_l_kernel(tc, x_words, x_scales, w1, pos1, pos2, pos
             nc.sync.dma_start(out=pair[:], in_=w_rows[:, 2 * u : 2 * u + 2, :])
             w_raw.append(pair)
         x_codes = keep.tile([P, 2 * T], U8, name="x_codes", align_bytes=64)
-        nc.sync.dma_start(out=x_codes[:].bitcast(I32), in_=x_words[0].bitcast(I32))
+        early, late = slice(0, T), slice(T, 2 * T)
+        nc.sync.dma_start(out=x_codes[:, early].bitcast(I32), in_=x_words[0, :, early].bitcast(I32))
         for q in range(4):
             nc.sync.dma_start(
                 out=x_plane[32 * q : 32 * q + 4, :].bitcast(I32),
                 in_=x_scales[0, 4 * q : 4 * q + 4, :].bitcast(I32),
             )
+        nc.sync.dma_start(out=x_codes[:, late].bitcast(I32), in_=x_words[0, :, late].bitcast(I32))
         lists = []
         for name, pos in (("pos1", pos1), ("pos2", pos2), ("pos3", pos3)):
             offsets = keep.tile([P, T // 16], U16, name=name)
@@ -58,7 +60,8 @@ def tile_picked_wmedian_relu_l_kernel(tc, x_words, x_scales, w1, pos1, pos2, pos
             lists.append(offsets)
 
         ident = keep.tile([P, P], F32, name="ident")
-        make_identity(nc, ident[:])
+        nc.vector.memset(ident[:], 0.0)
+        make_identity(nc, ident[:], nomemset=True)
 
         w_grouped = keep.tile([P, N, PACK], BF16, name="w_grouped", align_bytes=64)
         w_codes = keep.tile([P, N], U32, name="w_codes", align_bytes=64)

@@ -17,15 +17,13 @@ FP4X4 = mybir.dt.float4_e2m1fn_x4
 MAX = mybir.AluOpType.max
 MIN = mybir.AluOpType.min
 MULT = mybir.AluOpType.mult
-ADD = mybir.AluOpType.add
-SUB = mybir.AluOpType.subtract
-ABS = mybir.ActivationFunctionType.Abs
+COPY = mybir.ActivationFunctionType.Copy
 RELU = mybir.ActivationFunctionType.Relu
 
 P = 128
 PACK = 4
 HALF = T // 2
-SPARE = 32
+SPARE = 192
 CHUNKS = ((0, 192), (192, 384), (384, 512))
 
 
@@ -100,45 +98,51 @@ def tile_picked_wmedian_relu_l_kernel(tc, x_words, x_scales, w1, pos1, pos2, pos
             else:
                 nc.scalar.activation(out=y[:, cols], in_=acc[:], func=RELU)
 
-        neg0, n1, lo, rise, step, med, gap_t = (
-            keep.tile([P, T], F32, name=t) for t in ("neg0", "n1", "lo", "rise", "step", "med", "gap_t")
+        neg_a, b, c, lo, mid, med, a_t, rise_t = (
+            keep.tile([P, T], F32, name=t) for t in ("neg_a", "b", "c", "lo", "mid", "med", "a_t", "rise_t")
         )
         blocks = [slice(P * i, P * (i + 1)) for i in range(T // P)]
-        diff = [psum.tile([P, P], F32, name="diff%d" % i) for i in range(T // P)]
-        gap_early = psum.tile([P, T - P], F32, name="gap_early", tag="bank0")
-        gap_late = psum.tile([P, P], F32, name="gap_late", tag="bank1")
-
-        def gap(cols):
-            if cols.start < T - P:
-                return gap_early[:, cols]
-            return gap_late[:, cols.start - (T - P) : cols.stop - (T - P)]
-
-        def entries(window, offsets, cols):
-            return window.indirect(offsets[:, cols.start // 16 : cols.stop // 16])
-
         sides = (slice(0, HALF), slice(HALF, T))
-        nc.vector.tensor_tensor(out=neg0[:], in0=y[:].indirect(lists[0][:]), in1=minus_one[:], op=MULT)
-        for cols in (slice(0, T - P), slice(T - P, T)):
-            nc.vector.tensor_copy(out=n1[:, cols], in_=entries(y[:], lists[1], cols))
-        for i, cols in enumerate(blocks):
-            nc.tensor.matmul(diff[i][:], lhsT=neg0[:, cols], rhs=ident[:], start=True, stop=False, is_transpose=True)
-        for i, cols in enumerate(blocks):
-            nc.tensor.matmul(diff[i][:], lhsT=n1[:, cols], rhs=ident[:], start=False, stop=True, is_transpose=True)
-        for i, cols in enumerate(blocks):
-            nc.scalar.activation(out=gap_t[:, cols], in_=diff[i][:], func=ABS)
-            nc.tensor.transpose(gap(cols), gap_t[:, cols], ident[:])
-        for cols in sides:
-            nc.vector.scalar_tensor_tensor(out=lo[:, cols], in0=neg0[:, cols], scalar=-1.0, in1=n1[:, cols], op0=MULT, op1=MIN)
-        for cols in sides:
-            nc.vector.tensor_tensor(out=rise[:, cols], in0=entries(y[:], lists[2], cols), in1=lo[:, cols], op=SUB)
 
-        def middle(c):
-            cols = slice(*CHUNKS[c])
-            nc.vector.scalar_tensor_tensor(out=step[:, cols], in0=rise[:, cols], scalar=0.0, in1=gap(cols), op0=MAX, op1=MIN)
+        nc.vector.tensor_tensor(out=neg_a[:], in0=y[:].indirect(lists[0][:]), in1=minus_one[:], op=MULT)
+        nc.vector.tensor_copy(out=b[:], in_=y[:].indirect(lists[1][:]))
+        nc.vector.tensor_copy(out=c[:], in_=y[:].indirect(lists[2][:]))
 
-        def finish(c):
-            cols = slice(*CHUNKS[c])
-            nc.vector.tensor_tensor(out=med[:, cols], in0=lo[:, cols], in1=step[:, cols], op=ADD)
+        def turn(bank, src, start, stop):
+            nc.tensor.matmul(bank, lhsT=src, rhs=ident[:], start=start, stop=stop, is_transpose=True)
+
+        for i, cols in enumerate(blocks):
+            turned = psum.tile([P, P], F32, name="turned%d" % i, tag="bank%d" % i)
+            turn(turned[:], neg_a[:, cols], True, True)
+            nc.scalar.activation(out=a_t[:, cols], in_=turned[:], func=COPY, scale=-1.0)
+        diff = [psum.tile([P, P], F32, name="diff%d" % i, tag="diff%d" % i) for i in range(T // P)]
+        for i, cols in enumerate(blocks):
+            turn(diff[i][:], neg_a[:, cols], True, False)
+        for i, cols in enumerate(blocks):
+            turn(diff[i][:], b[:, cols], False, True)
+            nc.scalar.activation(out=rise_t[:, cols], in_=diff[i][:], func=RELU)
+        hi_early = psum.tile([P, T - P], F32, name="hi_early", tag="bank0")
+        hi_late = psum.tile([P, P], F32, name="hi_late", tag="diff3")
+        for i, cols in enumerate(blocks[:-1]):
+            turn(hi_early[:, cols], a_t[:, cols], i == 0, False)
+        for i, cols in enumerate(blocks[:-1]):
+            turn(hi_early[:, cols], rise_t[:, cols], False, i == len(blocks) - 2)
+        turn(hi_late[:], a_t[:, blocks[-1]], True, False)
+        turn(hi_late[:], rise_t[:, blocks[-1]], False, True)
+
+        def hi(cols):
+            return hi_early[:, cols] if cols.start < T - P else hi_late[:]
+
+        for cols in sides:
+            nc.vector.scalar_tensor_tensor(out=lo[:, cols], in0=neg_a[:, cols], scalar=-1.0, in1=b[:, cols], op0=MULT, op1=MIN)
+
+        def middle(n):
+            cols = slice(*CHUNKS[n])
+            nc.vector.tensor_tensor(out=mid[:, cols], in0=lo[:, cols], in1=c[:, cols], op=MAX)
+
+        def finish(n):
+            cols = slice(*CHUNKS[n])
+            nc.vector.tensor_tensor(out=med[:, cols], in0=mid[:, cols], in1=hi(cols), op=MIN)
             nc.sync.dma_start(out=out[:, cols], in_=med[:, cols])
 
         middle(0)

@@ -22,9 +22,9 @@ RELU = mybir.ActivationFunctionType.Relu
 
 P = 128
 PACK = 4
-HALF = T // 2
 SPARE = 192
-CHUNKS = ((0, 192), (192, 384), (384, 512))
+CHUNKS = ((0, 128), (128, 304), (304, 512))
+BANKS = ((0, 1), (1, 3), (3, 4))
 
 
 def tile_picked_wmedian_relu_l_kernel(tc, x_words, x_scales, w1, pos1, pos2, pos3, out):
@@ -102,7 +102,6 @@ def tile_picked_wmedian_relu_l_kernel(tc, x_words, x_scales, w1, pos1, pos2, pos
             keep.tile([P, T], F32, name=t) for t in ("neg_a", "b", "c", "lo", "mid", "med", "a_t", "rise_t")
         )
         blocks = [slice(P * i, P * (i + 1)) for i in range(T // P)]
-        sides = (slice(0, HALF), slice(HALF, T))
 
         nc.vector.tensor_tensor(out=neg_a[:], in0=y[:].indirect(lists[0][:]), in1=minus_one[:], op=MULT)
         nc.vector.tensor_copy(out=b[:], in_=y[:].indirect(lists[1][:]))
@@ -111,43 +110,44 @@ def tile_picked_wmedian_relu_l_kernel(tc, x_words, x_scales, w1, pos1, pos2, pos
         def turn(bank, src, start, stop):
             nc.tensor.matmul(bank, lhsT=src, rhs=ident[:], start=start, stop=stop, is_transpose=True)
 
-        for i, cols in enumerate(blocks):
+        def sign_turned(i):
             turned = psum.tile([P, P], F32, name="turned%d" % i, tag="bank%d" % i)
-            turn(turned[:], neg_a[:, cols], True, True)
-            nc.scalar.activation(out=a_t[:, cols], in_=turned[:], func=COPY, scale=-1.0)
+            turn(turned[:], neg_a[:, blocks[i]], True, True)
+            nc.scalar.activation(out=a_t[:, blocks[i]], in_=turned[:], func=COPY, scale=-1.0)
+
         diff = [psum.tile([P, P], F32, name="diff%d" % i, tag="diff%d" % i) for i in range(T // P)]
-        for i, cols in enumerate(blocks):
-            turn(diff[i][:], neg_a[:, cols], True, False)
-        for i, cols in enumerate(blocks):
-            turn(diff[i][:], b[:, cols], False, True)
-            nc.scalar.activation(out=rise_t[:, cols], in_=diff[i][:], func=RELU)
-        hi_early = psum.tile([P, T - P], F32, name="hi_early", tag="bank0")
-        hi_late = psum.tile([P, P], F32, name="hi_late", tag="diff3")
-        for i, cols in enumerate(blocks[:-1]):
-            turn(hi_early[:, cols], a_t[:, cols], i == 0, False)
-        for i, cols in enumerate(blocks[:-1]):
-            turn(hi_early[:, cols], rise_t[:, cols], False, i == len(blocks) - 2)
-        turn(hi_late[:], a_t[:, blocks[-1]], True, False)
-        turn(hi_late[:], rise_t[:, blocks[-1]], False, True)
 
-        def hi(cols):
-            return hi_early[:, cols] if cols.start < T - P else hi_late[:]
+        def close_diff(i):
+            turn(diff[i][:], b[:, blocks[i]], False, True)
+            nc.scalar.activation(out=rise_t[:, blocks[i]], in_=diff[i][:], func=RELU)
 
-        for cols in sides:
+        for i in range(T // P):
+            sign_turned(i)
+        for i in range(T // P):
+            turn(diff[i][:], neg_a[:, blocks[i]], True, False)
+        for i in range(T // P):
+            close_diff(i)
+        hi = []
+        for n, (first, last) in enumerate(BANKS):
+            tag = "diff%d" % first if last == T // P else "bank%d" % first
+            bank = psum.tile([P, P * (last - first)], F32, name="hi%d" % n, tag=tag)
+            for i in range(first, last):
+                turn(bank[:, blocks[i - first]], a_t[:, blocks[i]], i == first, False)
+            for i in range(first, last):
+                turn(bank[:, blocks[i - first]], rise_t[:, blocks[i]], False, i == last - 1)
+            hi.append((P * first, P * last, bank))
+
+        for first, last in CHUNKS:
+            cols = slice(first, last)
             nc.vector.scalar_tensor_tensor(out=lo[:, cols], in0=neg_a[:, cols], scalar=-1.0, in1=b[:, cols], op0=MULT, op1=MIN)
-
-        def middle(n):
-            cols = slice(*CHUNKS[n])
+        for first, last in CHUNKS:
+            cols = slice(first, last)
             nc.vector.tensor_tensor(out=mid[:, cols], in0=lo[:, cols], in1=c[:, cols], op=MAX)
-
-        def finish(n):
-            cols = slice(*CHUNKS[n])
-            nc.vector.tensor_tensor(out=med[:, cols], in0=mid[:, cols], in1=hi(cols), op=MIN)
-            nc.sync.dma_start(out=out[:, cols], in_=med[:, cols])
-
-        middle(0)
-        middle(1)
-        finish(0)
-        middle(2)
-        finish(1)
-        finish(2)
+        for first, last in CHUNKS:
+            for begin, end, bank in hi:
+                left, right = max(first, begin), min(last, end)
+                if left < right:
+                    nc.vector.tensor_tensor(
+                        out=med[:, left:right], in0=mid[:, left:right], in1=bank[:, left - begin : right - begin], op=MIN
+                    )
+            nc.sync.dma_start(out=out[:, first:last], in_=med[:, first:last])

@@ -17,14 +17,13 @@ FP4X4 = mybir.dt.float4_e2m1fn_x4
 MAX = mybir.AluOpType.max
 MIN = mybir.AluOpType.min
 MULT = mybir.AluOpType.mult
-COPY = mybir.ActivationFunctionType.Copy
 RELU = mybir.ActivationFunctionType.Relu
 
 P = 128
 PACK = 4
 SPARE = 192
-CHUNKS = ((0, 128), (128, 304), (304, 512))
-BANKS = ((0, 1), (1, 3), (3, 4))
+CHUNKS = ((0, 160), (160, 336), (336, 512))
+BANKS = ((0, 2), (2, 4))
 
 
 def tile_picked_wmedian_relu_l_kernel(tc, x_words, x_scales, w1, pos1, pos2, pos3, out):
@@ -98,38 +97,38 @@ def tile_picked_wmedian_relu_l_kernel(tc, x_words, x_scales, w1, pos1, pos2, pos
             else:
                 nc.scalar.activation(out=y[:, cols], in_=acc[:], func=RELU)
 
-        neg_a, b, c, lo, mid, med, a_t, rise_t = (
-            keep.tile([P, T], F32, name=t) for t in ("neg_a", "b", "c", "lo", "mid", "med", "a_t", "rise_t")
+        a, neg_b, c, lo, mid, med, a_t, rise_t = (
+            keep.tile([P, T], F32, name=t) for t in ("a", "neg_b", "c", "lo", "mid", "med", "a_t", "rise_t")
         )
         blocks = [slice(P * i, P * (i + 1)) for i in range(T // P)]
 
-        nc.vector.tensor_tensor(out=neg_a[:], in0=y[:].indirect(lists[0][:]), in1=minus_one[:], op=MULT)
-        nc.vector.tensor_copy(out=b[:], in_=y[:].indirect(lists[1][:]))
+        nc.vector.tensor_copy(out=a[:], in_=y[:].indirect(lists[0][:]))
+        nc.vector.tensor_tensor(out=neg_b[:], in0=y[:].indirect(lists[1][:]), in1=minus_one[:], op=MULT)
         nc.vector.tensor_copy(out=c[:], in_=y[:].indirect(lists[2][:]))
 
         def turn(bank, src, start, stop):
             nc.tensor.matmul(bank, lhsT=src, rhs=ident[:], start=start, stop=stop, is_transpose=True)
 
-        def sign_turned(i):
+        def turn_a(i):
             turned = psum.tile([P, P], F32, name="turned%d" % i, tag="bank%d" % i)
-            turn(turned[:], neg_a[:, blocks[i]], True, True)
-            nc.scalar.activation(out=a_t[:, blocks[i]], in_=turned[:], func=COPY, scale=-1.0)
+            turn(turned[:], a[:, blocks[i]], True, True)
+            nc.scalar.copy(out=a_t[:, blocks[i]], in_=turned[:])
 
         diff = [psum.tile([P, P], F32, name="diff%d" % i, tag="diff%d" % i) for i in range(T // P)]
 
         def close_diff(i):
-            turn(diff[i][:], b[:, blocks[i]], False, True)
-            nc.scalar.activation(out=rise_t[:, blocks[i]], in_=diff[i][:], func=RELU)
+            turn(diff[i][:], neg_b[:, blocks[i]], False, True)
+            nc.scalar.activation(out=rise_t[:, blocks[i]], in_=diff[i][:], func=RELU, scale=-1.0)
 
         for i in range(T // P):
-            sign_turned(i)
+            turn_a(i)
         for i in range(T // P):
-            turn(diff[i][:], neg_a[:, blocks[i]], True, False)
+            turn(diff[i][:], a[:, blocks[i]], True, False)
         for i in range(T // P):
             close_diff(i)
         hi = []
         for n, (first, last) in enumerate(BANKS):
-            tag = "diff%d" % first if last == T // P else "bank%d" % first
+            tag = "bank%d" % first
             bank = psum.tile([P, P * (last - first)], F32, name="hi%d" % n, tag=tag)
             for i in range(first, last):
                 turn(bank[:, blocks[i - first]], a_t[:, blocks[i]], i == first, False)
@@ -139,7 +138,7 @@ def tile_picked_wmedian_relu_l_kernel(tc, x_words, x_scales, w1, pos1, pos2, pos
 
         for first, last in CHUNKS:
             cols = slice(first, last)
-            nc.vector.scalar_tensor_tensor(out=lo[:, cols], in0=neg_a[:, cols], scalar=-1.0, in1=b[:, cols], op0=MULT, op1=MIN)
+            nc.vector.scalar_tensor_tensor(out=lo[:, cols], in0=neg_b[:, cols], scalar=-1.0, in1=a[:, cols], op0=MULT, op1=MIN)
         for first, last in CHUNKS:
             cols = slice(first, last)
             nc.vector.tensor_tensor(out=mid[:, cols], in0=lo[:, cols], in1=c[:, cols], op=MAX)

@@ -23,7 +23,7 @@ P = 128
 PACK = 4
 SPARE = 192
 CHUNKS = ((0, 160), (160, 336), (336, 512))
-BANKS = ((0, 2), (2, 4))
+BANKS = ((0, 2), (2, 3), (3, 4))
 
 
 def tile_picked_wmedian_relu_l_kernel(tc, x_words, x_scales, w1, pos1, pos2, pos3, out):
@@ -128,7 +128,7 @@ def tile_picked_wmedian_relu_l_kernel(tc, x_words, x_scales, w1, pos1, pos2, pos
             close_diff(i)
         hi = []
         for n, (first, last) in enumerate(BANKS):
-            tag = "bank%d" % first
+            tag = "bank0" if first == 0 else "diff%d" % first
             bank = psum.tile([P, P * (last - first)], F32, name="hi%d" % n, tag=tag)
             for i in range(first, last):
                 turn(bank[:, blocks[i - first]], a_t[:, blocks[i]], i == first, False)

@@ -22,7 +22,7 @@ RELU = mybir.ActivationFunctionType.Relu
 P = 128
 PACK = 4
 SPARE = 192
-CHUNKS = ((0, 160), (160, 336), (336, 512))
+CHUNKS = ((0, 128), (128, 320), (320, 512))
 BANKS = ((0, 2), (2, 3), (3, 4))
 
 

@@ -80,7 +80,7 @@ def tile_picked_wmedian_relu_l_kernel(tc, x_words, x_scales, w1, pos1, pos2, pos
         nc.vector.memset(y[:, T:], 0.0)
         minus_one = keep.tile([P, T], F32, name="minus_one")
         nc.vector.memset(minus_one[:], -1.0)
-        for h, (a, b, eng) in enumerate(((0, 128, "v"), (128, 256, "s"), (256, 384, "v"), (384, 512, "s"))):
+        for h, (a, b, eng) in enumerate(((0, 256, "s"), (256, 384, "v"), (384, 512, "s"))):
             cols = slice(a, b)
             acc = psum.tile([P, b - a], F32, name="acc%d" % h, tag="bank%d" % h)
             nc.tensor.matmul_mx(

@@ -1,7 +1,6 @@
 from contextlib import ExitStack
 
 import concourse.mybir as mybir
-from concourse.masks import make_identity
 
 K, T, N = 512, 512, 128
 FLOPS = 2 * K * T * N
@@ -16,14 +15,15 @@ FP8X4 = mybir.dt.float8_e4m3fn_x4
 FP4X4 = mybir.dt.float4_e2m1fn_x4
 MAX = mybir.AluOpType.max
 MIN = mybir.AluOpType.min
-MULT = mybir.AluOpType.mult
 RELU = mybir.ActivationFunctionType.Relu
+COPY = mybir.ActivationFunctionType.Copy
 
 P = 128
 PACK = 4
-SPARE = 192
+GROUP = 16
+PASSES = ((0, 256, "s"), (256, 384, "v"), (384, 512, "s"))
 CHUNKS = ((0, 128), (128, 320), (320, 512))
-BANKS = ((0, 2), (2, 3), (3, 4))
+PARTS = ((0, 320), (320, 512))
 
 
 def tile_picked_wmedian_relu_l_kernel(tc, x_words, x_scales, w1, pos1, pos2, pos3, out):
@@ -52,13 +52,9 @@ def tile_picked_wmedian_relu_l_kernel(tc, x_words, x_scales, w1, pos1, pos2, pos
         nc.sync.dma_start(out=x_codes[:, late].bitcast(I32), in_=x_words[0, :, late].bitcast(I32))
         lists = []
         for name, pos in (("pos1", pos1), ("pos2", pos2), ("pos3", pos3)):
-            offsets = keep.tile([P, T // 16], U16, name=name)
+            offsets = keep.tile([P, T // GROUP], U16, name=name)
             nc.sync.dma_start(offsets[:], pos)
             lists.append(offsets)
-
-        ident = keep.tile([P, P], F32, name="ident")
-        nc.vector.memset(ident[:], 0.0)
-        make_identity(nc, ident[:], nomemset=True)
 
         w_grouped = keep.tile([P, N, PACK], BF16, name="w_grouped", align_bytes=64)
         w_codes = keep.tile([P, N], U32, name="w_codes", align_bytes=64)
@@ -76,13 +72,10 @@ def tile_picked_wmedian_relu_l_kernel(tc, x_words, x_scales, w1, pos1, pos2, pos
                 in_=w_grouped[:, m, :].rearrange("p m t -> p (m t)"),
             )
 
-        y = keep.tile([P, T + SPARE], F32, name="y")
-        nc.vector.memset(y[:, T:], 0.0)
-        minus_one = keep.tile([P, T], F32, name="minus_one")
-        nc.vector.memset(minus_one[:], -1.0)
-        for h, (a, b, eng) in enumerate(((0, 256, "s"), (256, 384, "v"), (384, 512, "s"))):
-            cols = slice(a, b)
-            acc = psum.tile([P, b - a], F32, name="acc%d" % h, tag="bank%d" % h)
+        y = keep.tile([P, T], F32, name="y")
+        for h, (first, last, eng) in enumerate(PASSES):
+            cols = slice(first, last)
+            acc = psum.tile([P, last - first], F32, name="acc%d" % h, tag="bank%d" % h)
             nc.tensor.matmul_mx(
                 out=acc[:],
                 lhsT=w_codes[:].bitcast(FP8X4),
@@ -97,56 +90,31 @@ def tile_picked_wmedian_relu_l_kernel(tc, x_words, x_scales, w1, pos1, pos2, pos
             else:
                 nc.scalar.activation(out=y[:, cols], in_=acc[:], func=RELU)
 
-        a, neg_b, c, lo, mid, med, a_t, rise_t = (
-            keep.tile([P, T], F32, name=t) for t in ("a", "neg_b", "c", "lo", "mid", "med", "a_t", "rise_t")
-        )
-        blocks = [slice(P * i, P * (i + 1)) for i in range(T // P)]
+        a, b, c, lo, hi, mid, med = (keep.tile([P, T], F32, name=t) for t in ("a", "b", "c", "lo", "hi", "mid", "med"))
 
-        nc.vector.tensor_copy(out=a[:], in_=y[:].indirect(lists[0][:]))
-        nc.vector.tensor_tensor(out=neg_b[:], in0=y[:].indirect(lists[1][:]), in1=minus_one[:], op=MULT)
-        nc.vector.tensor_copy(out=c[:], in_=y[:].indirect(lists[2][:]))
+        def picked(n, first, last):
+            return y[:].indirect(lists[n][:, first // GROUP : last // GROUP])
 
-        def turn(bank, src, start, stop):
-            nc.tensor.matmul(bank, lhsT=src, rhs=ident[:], start=start, stop=stop, is_transpose=True)
+        def gather_v(dst, n, first, last):
+            nc.vector.tensor_copy(out=dst[:, first:last], in_=picked(n, first, last))
 
-        def turn_a(i):
-            turned = psum.tile([P, P], F32, name="turned%d" % i, tag="bank%d" % i)
-            turn(turned[:], a[:, blocks[i]], True, True)
-            nc.scalar.copy(out=a_t[:, blocks[i]], in_=turned[:])
+        def gather_s(dst, n, first, last):
+            nc.scalar.activation(out=dst[:, first:last], in_=picked(n, first, last), func=COPY)
 
-        diff = [psum.tile([P, P], F32, name="diff%d" % i, tag="diff%d" % i) for i in range(T // P)]
+        def pick(dst, left, right, op, first, last):
+            nc.vector.tensor_tensor(out=dst[:, first:last], in0=left[:, first:last], in1=right[:, first:last], op=op)
 
-        def close_diff(i):
-            turn(diff[i][:], neg_b[:, blocks[i]], False, True)
-            nc.scalar.activation(out=rise_t[:, blocks[i]], in_=diff[i][:], func=RELU, scale=-1.0)
-
-        for i in range(T // P):
-            turn_a(i)
-        for i in range(T // P):
-            turn(diff[i][:], a[:, blocks[i]], True, False)
-        for i in range(T // P):
-            close_diff(i)
-        hi = []
-        for n, (first, last) in enumerate(BANKS):
-            tag = "bank0" if first == 0 else "diff%d" % first
-            bank = psum.tile([P, P * (last - first)], F32, name="hi%d" % n, tag=tag)
-            for i in range(first, last):
-                turn(bank[:, blocks[i - first]], a_t[:, blocks[i]], i == first, False)
-            for i in range(first, last):
-                turn(bank[:, blocks[i - first]], rise_t[:, blocks[i]], False, i == last - 1)
-            hi.append((P * first, P * last, bank))
-
+        for first, last in PARTS:
+            gather_v(b, 1, first, last)
+        for first, last in PARTS:
+            gather_s(a, 0, first, last)
+        for first, last in PARTS:
+            gather_s(c, 2, first, last)
+        for first, last in PARTS:
+            pick(lo, a, b, MIN, first, last)
+            pick(hi, a, b, MAX, first, last)
+        for first, last in PARTS:
+            pick(mid, lo, c, MAX, first, last)
         for first, last in CHUNKS:
-            cols = slice(first, last)
-            nc.vector.scalar_tensor_tensor(out=lo[:, cols], in0=neg_b[:, cols], scalar=-1.0, in1=a[:, cols], op0=MULT, op1=MIN)
-        for first, last in CHUNKS:
-            cols = slice(first, last)
-            nc.vector.tensor_tensor(out=mid[:, cols], in0=lo[:, cols], in1=c[:, cols], op=MAX)
-        for first, last in CHUNKS:
-            for begin, end, bank in hi:
-                left, right = max(first, begin), min(last, end)
-                if left < right:
-                    nc.vector.tensor_tensor(
-                        out=med[:, left:right], in0=mid[:, left:right], in1=bank[:, left - begin : right - begin], op=MIN
-                    )
+            pick(med, mid, hi, MIN, first, last)
             nc.sync.dma_start(out=out[:, first:last], in_=med[:, first:last])

@@ -22,8 +22,8 @@ P = 128
 PACK = 4
 GROUP = 16
 PASSES = ((0, 256, "s"), (256, 384, "v"), (384, 512, "s"))
-CHUNKS = ((0, 128), (128, 320), (320, 512))
 PARTS = ((0, 320), (320, 512))
+THIRDS = ((0, 256), (256, 384), (384, 512))
 
 
 def tile_picked_wmedian_relu_l_kernel(tc, x_words, x_scales, w1, pos1, pos2, pos3, out):
@@ -104,17 +104,23 @@ def tile_picked_wmedian_relu_l_kernel(tc, x_words, x_scales, w1, pos1, pos2, pos
         def pick(dst, left, right, op, first, last):
             nc.vector.tensor_tensor(out=dst[:, first:last], in0=left[:, first:last], in1=right[:, first:last], op=op)
 
+        def finish(first, last):
+            pick(med, mid, hi, MIN, first, last)
+            nc.sync.dma_start(out=out[:, first:last], in_=med[:, first:last])
+
         for first, last in PARTS:
             gather_v(b, 1, first, last)
         for first, last in PARTS:
             gather_s(a, 0, first, last)
-        for first, last in PARTS:
+        for first, last in THIRDS:
             gather_s(c, 2, first, last)
-        for first, last in PARTS:
-            pick(lo, a, b, MIN, first, last)
-            pick(hi, a, b, MAX, first, last)
-        for first, last in PARTS:
-            pick(mid, lo, c, MAX, first, last)
-        for first, last in CHUNKS:
-            pick(med, mid, hi, MIN, first, last)
-            nc.sync.dma_start(out=out[:, first:last], in_=med[:, first:last])
+        pick(lo, a, b, MIN, *PARTS[0])
+        pick(hi, a, b, MAX, *PARTS[0])
+        pick(lo, a, b, MIN, *PARTS[1])
+        pick(mid, lo, c, MAX, *THIRDS[0])
+        pick(hi, a, b, MAX, *PARTS[1])
+        pick(mid, lo, c, MAX, *THIRDS[1])
+        finish(0, 128)
+        pick(mid, lo, c, MAX, *THIRDS[2])
+        finish(128, 384)
+        finish(384, 512)

@@ -120,7 +120,7 @@ def tile_picked_wmedian_relu_l_kernel(tc, x_words, x_scales, w1, pos1, pos2, pos
         pick(mid, lo, c, MAX, *THIRDS[0])
         pick(hi, a, b, MAX, *PARTS[1])
         pick(mid, lo, c, MAX, *THIRDS[1])
-        finish(0, 128)
+        finish(0, 192)
         pick(mid, lo, c, MAX, *THIRDS[2])
-        finish(128, 384)
+        finish(192, 384)
         finish(384, 512)

@@ -62,8 +62,8 @@ def tile_picked_wmedian_relu_l_kernel(tc, x_words, x_scales, w1, pos1, pos2, pos
         halves = (slice(0, N // 2), slice(N // 2, N))
         for u, m in ((0, slice(0, N)), (1, halves[0]), (1, halves[1])):
             nc.vector.tensor_copy(
-                out=w_grouped[:, m, 2 * u : 2 * u + 2].rearrange("p (c i) t -> p c t i", i=4),
-                in_=w_raw[u][:, :, m].rearrange("p t (c i) -> p c t i", i=4),
+                out=w_grouped[:, m, 2 * u : 2 * u + 2],
+                in_=w_raw[u][:, :, m].rearrange("p t m -> p m t"),
             )
         for m in halves:
             nc.vector.quantize_mx(

@@ -22,8 +22,6 @@ P = 128
 PACK = 4
 GROUP = 16
 PASSES = ((0, 256, "s"), (256, 384, "v"), (384, 512, "s"))
-PARTS = ((0, 320), (320, 512))
-THIRDS = ((0, 256), (256, 384), (384, 512))
 
 
 def tile_picked_wmedian_relu_l_kernel(tc, x_words, x_scales, w1, pos1, pos2, pos3, out):
@@ -108,19 +106,20 @@ def tile_picked_wmedian_relu_l_kernel(tc, x_words, x_scales, w1, pos1, pos2, pos
             pick(med, mid, hi, MIN, first, last)
             nc.sync.dma_start(out=out[:, first:last], in_=med[:, first:last])
 
-        for first, last in PARTS:
-            gather_v(b, 1, first, last)
-        for first, last in PARTS:
-            gather_s(a, 0, first, last)
-        for first, last in THIRDS:
-            gather_s(c, 2, first, last)
-        pick(lo, a, b, MIN, *PARTS[0])
-        pick(hi, a, b, MAX, *PARTS[0])
-        pick(lo, a, b, MIN, *PARTS[1])
-        pick(mid, lo, c, MAX, *THIRDS[0])
-        pick(hi, a, b, MAX, *PARTS[1])
-        pick(mid, lo, c, MAX, *THIRDS[1])
+        gather_v(b, 1, 0, 352)
+        gather_v(b, 1, 352, 512)
+        gather_s(a, 0, 0, 352)
+        gather_s(a, 0, 352, 512)
+        gather_s(c, 2, 0, 224)
+        gather_s(c, 2, 224, 384)
+        gather_s(c, 2, 384, 512)
+        pick(lo, a, b, MIN, 0, 352)
+        pick(hi, a, b, MAX, 0, 352)
+        pick(lo, a, b, MIN, 352, 512)
+        pick(mid, lo, c, MAX, 0, 224)
+        pick(hi, a, b, MAX, 352, 512)
+        pick(mid, lo, c, MAX, 224, 384)
         finish(0, 192)
-        pick(mid, lo, c, MAX, *THIRDS[2])
+        pick(mid, lo, c, MAX, 384, 512)
         finish(192, 384)
         finish(384, 512)

from contextlib import ExitStack

import concourse.mybir as mybir

K, T, N = 512, 512, 128
FLOPS = 2 * K * T * N

F32 = mybir.dt.float32
BF16 = mybir.dt.bfloat16
I32 = mybir.dt.int32
U32 = mybir.dt.uint32
U16 = mybir.dt.uint16
U8 = mybir.dt.uint8
FP8X4 = mybir.dt.float8_e4m3fn_x4
FP4X4 = mybir.dt.float4_e2m1fn_x4
MAX = mybir.AluOpType.max
MIN = mybir.AluOpType.min
RELU = mybir.ActivationFunctionType.Relu
COPY = mybir.ActivationFunctionType.Copy

P = 128
PACK = 4
GROUP = 16
PASSES = ((0, 256, "s"), (256, 384, "v"), (384, 512, "s"))


def tile_picked_wmedian_relu_l_kernel(tc, x_words, x_scales, w1, pos1, pos2, pos3, out):
    nc = tc.nc
    with ExitStack() as ctx:
        keep = ctx.enter_context(tc.tile_pool(name="keep", bufs=1))
        psum = ctx.enter_context(tc.psum_pool(name="psum", bufs=1))

        x_plane = keep.tile([P, T], U8, name="x_plane", align_bytes=64)
        nc.vector.memset(x_plane[:].bitcast(I32), 0)

        w_rows = w1.rearrange("(p j) m -> p j m", j=PACK)
        w_raw = []
        for u in range(2):
            pair = keep.tile([P, 2, N], F32, name="w_raw%d" % u)
            nc.sync.dma_start(out=pair[:], in_=w_rows[:, 2 * u : 2 * u + 2, :])
            w_raw.append(pair)
        x_codes = keep.tile([P, 2 * T], U8, name="x_codes", align_bytes=64)
        early, late = slice(0, T), slice(T, 2 * T)
        nc.sync.dma_start(out=x_codes[:, early].bitcast(I32), in_=x_words[0, :, early].bitcast(I32))
        for q in range(4):
            nc.sync.dma_start(
                out=x_plane[32 * q : 32 * q + 4, :].bitcast(I32),
                in_=x_scales[0, 4 * q : 4 * q + 4, :].bitcast(I32),
            )
        nc.sync.dma_start(out=x_codes[:, late].bitcast(I32), in_=x_words[0, :, late].bitcast(I32))
        lists = []
        for name, pos in (("pos1", pos1), ("pos2", pos2), ("pos3", pos3)):
            offsets = keep.tile([P, T // GROUP], U16, name=name)
            nc.sync.dma_start(offsets[:], pos)
            lists.append(offsets)

        w_grouped = keep.tile([P, N, PACK], BF16, name="w_grouped", align_bytes=64)
        w_codes = keep.tile([P, N], U32, name="w_codes", align_bytes=64)
        w_plane = keep.tile([P, N], U8, name="w_plane", align_bytes=64)
        halves = (slice(0, N // 2), slice(N // 2, N))
        for u, m in ((0, slice(0, N)), (1, halves[0]), (1, halves[1])):
            nc.vector.tensor_copy(
                out=w_grouped[:, m, 2 * u : 2 * u + 2],
                in_=w_raw[u][:, :, m].rearrange("p t m -> p m t"),
            )
        for m in halves:
            nc.vector.quantize_mx(
                out=w_codes[:, m].bitcast(FP8X4),
                scales=w_plane[:, m],
                in_=w_grouped[:, m, :].rearrange("p m t -> p (m t)"),
            )

        y = keep.tile([P, T], F32, name="y")
        for h, (first, last, eng) in enumerate(PASSES):
            cols = slice(first, last)
            acc = psum.tile([P, last - first], F32, name="acc%d" % h, tag="bank%d" % h)
            nc.tensor.matmul_mx(
                out=acc[:],
                lhsT=w_codes[:].bitcast(FP8X4),
                lhsT_scale=w_plane[:],
                rhs=x_codes[:, 2 * cols.start : 2 * cols.stop].bitcast(FP4X4),
                rhs_scale=x_plane[:, cols],
                start=True,
                stop=True,
            )
            if eng == "v":
                nc.vector.tensor_scalar_max(out=y[:, cols], in0=acc[:], scalar1=0.0)
            else:
                nc.scalar.activation(out=y[:, cols], in_=acc[:], func=RELU)

        a, b, c, lo, hi, mid, med = (keep.tile([P, T], F32, name=t) for t in ("a", "b", "c", "lo", "hi", "mid", "med"))

        def picked(n, first, last):
            return y[:].indirect(lists[n][:, first // GROUP : last // GROUP])

        def gather_v(dst, n, first, last):
            nc.vector.tensor_copy(out=dst[:, first:last], in_=picked(n, first, last))

        def gather_s(dst, n, first, last):
            nc.scalar.activation(out=dst[:, first:last], in_=picked(n, first, last), func=COPY)

        def pick(dst, left, right, op, first, last):
            nc.vector.tensor_tensor(out=dst[:, first:last], in0=left[:, first:last], in1=right[:, first:last], op=op)

        def finish(first, last):
            pick(med, mid, hi, MIN, first, last)
            nc.sync.dma_start(out=out[:, first:last], in_=med[:, first:last])

        gather_v(b, 1, 0, 352)
        gather_v(b, 1, 352, 512)
        gather_s(a, 0, 0, 352)
        gather_s(a, 0, 352, 512)
        gather_s(c, 2, 0, 224)
        gather_s(c, 2, 224, 384)
        gather_s(c, 2, 384, 512)
        pick(lo, a, b, MIN, 0, 352)
        pick(hi, a, b, MAX, 0, 352)
        pick(lo, a, b, MIN, 352, 512)
        pick(mid, lo, c, MAX, 0, 224)
        pick(hi, a, b, MAX, 352, 512)
        pick(mid, lo, c, MAX, 224, 384)
        finish(0, 192)
        pick(mid, lo, c, MAX, 384, 512)
        finish(192, 384)
        finish(384, 512)
